import numpy as np
import ml_dtypes


def mxq(x, axis, fmt="e4m3"):
    dtype, down = {"e4m3": (ml_dtypes.float8_e4m3fn, 7), "e5m2": (ml_dtypes.float8_e5m2, 14)}[fmt]
    v = np.moveaxis(np.asarray(x, np.float32).astype(ml_dtypes.bfloat16).astype(np.float64), axis, -1)
    blocks = v.reshape(v.shape[:-1] + (-1, 32))
    amax = np.abs(blocks).max(-1, keepdims=True)
    byte = np.maximum(np.where(amax > 0, np.frexp(amax)[1] - 1 + 127, 0) - down, 1)
    scale = np.exp2(byte - 127.0)
    codes = (blocks / scale).astype(np.float32).astype(dtype).astype(np.float64)
    return np.moveaxis((codes * scale).reshape(v.shape), -1, axis)


WIDE = False


def mx_kscale(k):
    if not WIDE:
        return np.ones(k)
    levels = np.array([10, -10, 5, -5, 0])
    if k % 512:
        return np.exp2(np.random.permutation(np.resize(levels, k // 32))).repeat(32)
    a = np.empty((k // 512, 16))
    for p in range(k // 512):
        a[p, :8] = np.random.permutation(np.resize(levels, 8))
        for g in range(8):
            far = levels[np.abs(levels - a[p, g]) >= 10]
            a[p, g + 8] = far[np.random.randint(len(far))]
    return np.exp2(a.ravel()).repeat(32)


def f64(x):
    return np.asarray(x).astype(np.float64)


def striped(idx):
    return np.tile(idx.reshape(-1, 16).T, (8, 1)).astype(np.uint16)


def unstriped(offs):
    return offs[:16].T.reshape(-1).astype(np.int64)


def striped8(idx):
    return np.concatenate([x.reshape(-1, 16).T for x in idx]).astype(np.uint16)


def runs(offs, k):
    lists = np.stack([offs[16 * r : 16 * r + 16].T.reshape(-1) for r in range(8)]).astype(np.int64)
    return lists[np.arange(k) % 512 // 64]


def pack_weight(w):
    k, n = w.shape
    w = f64(np.asarray(w, np.float32).astype(ml_dtypes.bfloat16)).reshape(k // 32, 32, n)
    amax = np.abs(w).max(1)
    byte = np.clip(np.where(amax > 0, np.frexp(amax)[1] - 1 + 127 - 7, 1), 1, 254)
    scaled = (w * np.exp2(127.0 - byte)[:, None, :]).reshape(k, n).astype(np.float32)
    words = np.ascontiguousarray(scaled.reshape(k // 512, 128, 4, n).transpose(0, 1, 3, 2)).astype(ml_dtypes.float8_e4m3fn).view(np.uint8)
    return words, np.ascontiguousarray(byte.astype(np.uint8).reshape(k // 512, 16, n))


def unpack_weight(words, scales):
    g, p, n, _ = words.shape
    vals = np.ascontiguousarray(words).view(ml_dtypes.float8_e4m3fn).astype(np.float64) * np.repeat(np.exp2(scales.astype(np.float64) - 127.0), 8, axis=1)[..., None]
    return vals.transpose(0, 1, 3, 2).reshape(g * 512, n)


E2M1 = np.array([0.0, 0.5, 1.0, 1.5, 2.0, 3.0, 4.0, 6.0, -0.0, -0.5, -1.0, -1.5, -2.0, -3.0, -4.0, -6.0])


def pack_fp4(w):
    k, n = w.shape
    w = f64(np.asarray(w, np.float32).astype(ml_dtypes.bfloat16)).reshape(k // 32, 32, n)
    amax = np.abs(w).max(1)
    mant, ex = np.frexp(amax / 6.0)
    byte = np.clip(np.where(amax > 0, np.where(mant > 0.5, ex, ex - 1) + 127, 1), 1, 254)
    scaled = (w * np.exp2(127.0 - byte)[:, None, :]).reshape(k, n).astype(np.float32)
    c = np.ascontiguousarray(scaled.reshape(k // 512, 128, 4, n).transpose(0, 1, 3, 2)).astype(ml_dtypes.float4_e2m1fn).view(np.uint8) & 0xF
    words = (c[..., 0::2] | (c[..., 1::2] << 4)).reshape(k // 512, 128, 2 * n)
    return np.ascontiguousarray(words), np.ascontiguousarray(byte.astype(np.uint8).reshape(k // 512, 16, n))


def unpack_fp4(words, scales):
    g, _, n = scales.shape
    words = np.ascontiguousarray(words).reshape(g, 128, n, 2)
    nib = np.empty((g, 128, n, 4), np.uint8)
    nib[..., 0::2] = words & 0xF
    nib[..., 1::2] = words >> 4
    vals = E2M1[nib] * np.repeat(np.exp2(scales.astype(np.float64) - 127.0), 8, axis=1)[..., None]
    return vals.transpose(0, 1, 3, 2).reshape(g * 512, n)


def sigmoid(v):
    return 1.0 / (1.0 + np.exp(-np.maximum(v, -700.0)))

def planes(y):
    n, m = y.shape
    v = y.astype(np.float32).astype(ml_dtypes.bfloat16).astype(np.float64).reshape(n // 32, 32, m)
    top = np.abs(v).max(1)
    byte = np.clip(np.where(top > 0, np.frexp(top)[1] - 1 + 127 - 7, 1), 1, 254)
    codes = (v * np.exp2(127.0 - byte)[:, None, :]).reshape(n, m).astype(np.float32).astype(ml_dtypes.float8_e4m3fn).view(np.uint8)
    words = codes.reshape(n // 512, 128, 4, m).transpose(0, 1, 3, 2)
    return np.ascontiguousarray(words), np.ascontiguousarray(byte.astype(np.uint8).reshape(n // 512, 16, m))


K, T, S, H, C = 512, 2048, 512, 512, 512


def setup_inputs():
    n = np.random.standard_normal
    s = mx_kscale(K)[:, None]
    packed_xT = pack_weight(n((K, T)) * s)
    packed_w1 = pack_fp4(n((K, H)) / np.sqrt(K) / s)
    packed_w2 = pack_fp4(n((K, H)) / np.sqrt(K) / s)
    return {
        "x_words": packed_xT[0],
        "x_scales": packed_xT[1],
        "w1_words": packed_w1[0],
        "w1_scales": packed_w1[1],
        "w2_words": packed_w2[0],
        "w2_scales": packed_w2[1],
        "gs": (np.random.uniform(0.5, 1.5, (K, 1)) / s).astype(np.float32),
        "offs": striped(np.random.permutation(T)[:S]),
        "two": striped(np.random.permutation(T)[:S]),
        "n1": striped8(np.stack([np.random.permutation(S) for _ in range(8)])),
        "n2": striped8(np.stack([np.random.permutation(S) for _ in range(8)])),
        "cand": striped(np.random.permutation(T)[:C]),
        "n3": striped8(np.stack([np.random.permutation(S) for _ in range(8)])),
    }


def reference(x_words, x_scales, w1_words, w1_scales, w2_words, w2_scales, gs, offs, two, n1, n2, cand, n3):
    x_cand = unpack_weight(x_words, x_scales)[:, unstriped(cand)]
    xq = unpack_weight(x_words, x_scales)[:, unstriped(offs)]
    y = unpack_fp4(w1_words, w1_scales).T @ xq
    x_two = unpack_weight(x_words, x_scales)[:, unstriped(two)]
    d = unpack_fp4(w2_words, w2_scales).T @ x_two
    z = f64(gs) * (y * (sigmoid(d[np.arange(H)[:, None], runs(n2, H)])) - (0.5 * (y[np.arange(H)[:, None], runs(n1, H)])))
    s = 0.0625 * ((x_cand.T @ mxq(z, 0, "e4m3")))
    st = s - (s[np.arange(C)[:, None], runs(n3, C)])
    out_0 = st - (0.5 * (st[np.arange(C)[:, None], runs(n3, C)]))
    return (out_0,) + planes(out_0)

@@ -1,0 +1,217 @@
+from contextlib import ExitStack
+
+import concourse.mybir as mybir
+
+K, T, S = 512, 2048, 512
+FLOPS = 3 * 2 * K * S * S
+
+F32 = mybir.dt.float32
+BF16 = mybir.dt.bfloat16
+I32 = mybir.dt.int32
+U32 = mybir.dt.uint32
+U16 = mybir.dt.uint16
+U8 = mybir.dt.uint8
+FP8X4 = mybir.dt.float8_e4m3fn_x4
+FP4X4 = mybir.dt.float4_e2m1fn_x4
+ALU = mybir.AluOpType
+ACT = mybir.ActivationFunctionType
+
+P = 128
+PACK = 4
+PER_COL = 16
+HALF = S // 2
+PIECES = ((0, 256), (256, 384), (384, 512))
+
+
+def tile_picked_twcgatebtwice_none_po_kernel(
+    tc, x_words, x_scales, w1_words, w1_scales, w2_words, w2_scales, gs, offs, two, n1, n2, cand, n3, out_0, out_1, out_2
+):
+    nc = tc.nc
+    with ExitStack() as ctx:
+        keep = ctx.enter_context(tc.tile_pool(name="keep", bufs=1))
+        psum = ctx.enter_context(tc.psum_pool(name="psum", bufs=1))
+
+        def sb(name, shape, dtype):
+            return keep.tile(shape, dtype, name=name, align_bytes=64)
+
+        def bank(b, name):
+            return psum.tile([P, S], F32, name=name, tag="bank%d" % b)
+
+        def load_list(name, src):
+            t = keep.tile([P, S // PER_COL], U16, name=name)
+            nc.sync.dma_start(t[:], src)
+            return t
+
+        def entries(lst, lo, hi):
+            return lst[:, lo // PER_COL : hi // PER_COL]
+
+        def load_scales(eng, plane, src, quadrants):
+            rows = src[0].bitcast(I32)
+            for q in quadrants:
+                four = rows[4 * q : 4 * q + 4, :]
+                eng.dma_start(
+                    plane[32 * q : 32 * q + 32, :].bitcast(I32), four.unsqueeze(0).to_broadcast([8, 4, four.shape[1]])
+                )
+
+        def deal(name, src, dtype, per_col):
+            dst = sb(name, [P, S * per_col], dtype)
+            nc.vector.tensor_copy(
+                dst[:].rearrange("p (t m b) -> p t m b", t=PACK, b=per_col),
+                src[:].rearrange("p (m t b) -> p t m b", t=PACK, b=per_col),
+            )
+            return dst
+
+        xs = sb("xs", [P, T], U8)
+        w2s = sb("w2s", [P, S], U8)
+        w1s = sb("w1s", [P, S], U8)
+        l_offs = load_list("l_offs", offs)
+        load_scales(nc.sync, xs, x_scales, (0, 1))
+        load_scales(nc.scalar, xs, x_scales, (2, 3))
+        w1w = sb("w1w", [P, 2 * S], U8)
+        nc.scalar.dma_start(w1w[:].bitcast(I32), w1_words[0].bitcast(I32))
+        l_two = load_list("l_two", two)
+        xw = sb("xw", [P, T], U32)
+        nc.scalar.dma_start(xw[:].bitcast(I32), x_words[0].rearrange("p n t -> p (n t)").bitcast(I32))
+        load_scales(nc.sync, w1s, w1_scales, range(4))
+        gain = sb("gain", [P, PACK], F32)
+        nc.sync.dma_start(gain[:], gs.rearrange("(p t) o -> p (t o)", t=PACK))
+        w2w = sb("w2w", [P, 2 * S], U8)
+        nc.sync.dma_start(w2w[:].bitcast(I32), w2_words[0].bitcast(I32))
+        load_scales(nc.sync, w2s, w2_scales, range(4))
+        l_cand = load_list("l_cand", cand)
+        l_n2 = load_list("l_n2", n2)
+        l_n1 = load_list("l_n1", n1)
+        l_n3 = load_list("l_n3", n3)
+
+        warm = sb("warm", [P, 2], F32)
+        nc.gpsimd.memset(warm[:, 0:1], 0.0)
+        warm2 = sb("warm2", [P, 2], F32)
+        nc.scalar.activation(warm2[:, 0:1], warm[:, 0:1], ACT.Sigmoid)
+
+        def pick(name, table, lst, dtype):
+            g = sb(name, [P, S], dtype)
+            nc.vector.tensor_copy(g[:], table[:].indirect(lst[:]))
+            return g
+
+        def project(name, first_bank, w_words, w_scales, g_words, g_scales):
+            banks = []
+            for t in range(PACK):
+                acc = bank(first_bank + t, "%s%d" % (name, t))
+                nc.tensor.matmul_mx(
+                    out=acc[:],
+                    lhsT=w_words[:, 2 * P * t : 2 * P * (t + 1)].bitcast(FP4X4),
+                    lhsT_scale=w_scales[:, P * t : P * (t + 1)],
+                    rhs=g_words[:].bitcast(FP8X4),
+                    rhs_scale=g_scales[:],
+                    start=True,
+                    stop=True,
+                )
+                banks.append(acc)
+            return banks
+
+        offs_s = pick("offs_s", xs, l_offs, U8)
+        w1w_d = deal("w1w_d", w1w, U8, 2)
+        offs_w = pick("offs_w", xw, l_offs, U32)
+        w1s_d = deal("w1s_d", w1s, U8, 1)
+        y_ps = project("y_ps", PACK, w1w_d, w1s_d, offs_w, offs_s)
+        two_s = pick("two_s", xs, l_two, U8)
+        two_w = pick("two_w", xw, l_two, U32)
+        w2w_d = deal("w2w_d", w2w, U8, 2)
+        w2s_d = deal("w2s_d", w2s, U8, 1)
+        d_ps = project("d_ps", 0, w2w_d, w2s_d, two_w, two_s)
+        cand_s = pick("cand_s", xs, l_cand, U8)
+        cand_w = pick("cand_w", xw, l_cand, U32)
+        cand_s_d = deal("cand_s_d", cand_s, U8, 1)
+        cand_w_d = deal("cand_w_d", cand_w, U32, 1)
+
+        s_win = [sb("s_win%d" % t, [P, 2 * S], F32) for t in range(PACK)]
+        y_win = [sb("y_win%d" % t, [P, S], F32) for t in range(PACK)]
+        gated = [sb("gated%d" % t, [P, S], F32) for t in range(PACK)]
+        d_win = [sb("d_win%d" % t, [P, S], F32) for t in range(PACK)]
+
+        def gate(t, lo, hi):
+            nc.scalar.activation(s_win[t][:, S + lo : S + hi], d_win[t][:].indirect(entries(l_n2, lo, hi)), ACT.Sigmoid)
+
+        for t in range(PACK):
+            nc.scalar.activation(y_win[t][:], y_ps[t][:], ACT.Copy, scale=gain[:, t : t + 1])
+        for pair in ((0, 1), (2, 3)):
+            for t in pair:
+                nc.scalar.copy(d_win[t][:], d_ps[t][:])
+            for t in pair:
+                gate(t, *PIECES[0])
+        for lo, hi in PIECES[1:]:
+            for t in range(PACK):
+                gate(t, lo, hi)
+
+        def interleave(eng, dst, src, scale):
+            o = dst[:].rearrange("p (c i t) -> p c t i", i=4, t=PACK)
+            i = src[:].rearrange("p t (c i) -> p c t i", i=4)
+            if eng is nc.scalar:
+                nc.scalar.activation(o, i, ACT.Copy, scale=scale)
+            else:
+                nc.vector.tensor_scalar(o, i, scale, None, ALU.mult)
+
+        zq = sb("zq", [P, S], U32)
+        zs = sb("zs", [P, S], U8)
+        s_ps = [[bank(t + PACK * h, "s_ps%d_%d" % (t, h)) for h in range(2)] for t in range(PACK)]
+        s_plain = [sb("s_plain%d" % t, [P, S], F32) for t in range(PACK)]
+        for n, (lo, hi) in enumerate(PIECES):
+            w = hi - lo
+            z2 = sb("z2_%d" % n, [P, PACK, w], F32)
+            for t in range(PACK):
+                nc.vector.scalar_tensor_tensor(
+                    gated[t][:, lo:hi], s_win[t][:, S + lo : S + hi], 2.0, y_win[t][:, lo:hi], ALU.mult, ALU.mult
+                )
+            for t in range(PACK):
+                nc.vector.tensor_tensor(
+                    z2[:, t, :], y_win[t][:].indirect(entries(l_n1, lo, hi)), gated[t][:, lo:hi], ALU.subtract
+                )
+            zb = sb("zb_%d" % n, [P, PACK * w], BF16)
+            interleave(nc.vector if n == len(PIECES) - 1 else nc.scalar, zb, z2, -0.5)
+            nc.vector.quantize_mx(out=zq[:, lo:hi].bitcast(FP8X4), scales=zs[:, lo:hi], in_=zb[:])
+            h = lo // HALF
+            for t in range(PACK):
+                nc.tensor.matmul_mx(
+                    out=s_ps[t][h][:, lo - h * HALF : hi - h * HALF],
+                    lhsT=cand_w_d[:, P * t : P * (t + 1)].bitcast(FP8X4),
+                    lhsT_scale=cand_s_d[:, P * t : P * (t + 1)],
+                    rhs=zq[:, lo:hi].bitcast(FP8X4),
+                    rhs_scale=zs[:, lo:hi],
+                    start=True,
+                    stop=True,
+                )
+            if hi % HALF == 0:
+                for t in range(PACK):
+                    for dst in (s_win[t], s_plain[t]):
+                        nc.scalar.activation(
+                            dst[:, h * HALF : (h + 1) * HALF], s_ps[t][h][:, 0:HALF], ACT.Copy, scale=0.03125
+                        )
+
+        st_win = [sb("st_win%d" % t, [P, S], F32) for t in range(PACK)]
+        st = [sb("st%d" % t, [P, S], F32) for t in range(PACK)]
+        for t in range(PACK):
+            nc.vector.tensor_tensor(st_win[t][:], s_win[t][:].indirect(l_n3[:]), s_plain[t][:], ALU.subtract)
+        for lo, hi in PIECES:
+            for t in range(PACK):
+                nc.scalar.activation(st[t][:, lo:hi], st_win[t][:, lo:hi], ACT.Copy, scale=-2.0)
+
+        oq = sb("oq", [P, S], U32)
+        osc = sb("osc", [P, S], U8)
+        out_rows = out_0.rearrange("(p t) c -> p t c", t=PACK)
+        out_words = out_1[0].rearrange("p n t -> p (n t)").bitcast(I32)
+        for n, (lo, hi) in enumerate(PIECES):
+            w = hi - lo
+            o = sb("o_%d" % n, [P, PACK, w], F32)
+            for t in range(PACK):
+                nc.vector.tensor_tensor(
+                    o[:, t, :], st_win[t][:].indirect(entries(l_n3, lo, hi)), st[t][:, lo:hi], ALU.add
+                )
+            nc.sync.dma_start(out_rows[:, :, lo:hi], o[:])
+            ob = sb("ob_%d" % n, [P, PACK * w], BF16)
+            interleave(nc.vector if n == len(PIECES) - 1 else nc.scalar, ob, o, 1.0)
+            nc.vector.quantize_mx(out=oq[:, lo:hi].bitcast(FP8X4), scales=osc[:, lo:hi], in_=ob[:])
+            nc.sync.dma_start(out_words[:, lo:hi], oq[:, lo:hi].bitcast(I32))
+        scale_rows = out_2[0].bitcast(I32)
+        for q in range(4):
+            eng = nc.sync if q % 2 == 0 else nc.scalar
+            eng.dma_start(scale_rows[4 * q : 4 * q + 4, :], osc[32 * q : 32 * q + 4, :].bitcast(I32))

@@ -20,7 +20,8 @@ P = 128
 PACK = 4
 PER_COL = 16
 HALF = S // 2
-PIECES = ((0, 256), (256, 384), (384, 512))
+PIECES = ((0, 256), (256, 512))
+CUT = 384
 
 
 def tile_picked_twcgatebtwice_none_po_kernel(
@@ -31,8 +32,8 @@ def tile_picked_twcgatebtwice_none_po_kernel(
         keep = ctx.enter_context(tc.tile_pool(name="keep", bufs=1))
         psum = ctx.enter_context(tc.psum_pool(name="psum", bufs=1))
 
-        def sb(name, shape, dtype):
-            return keep.tile(shape, dtype, name=name, align_bytes=64)
+        def sb(name, shape, dtype, tag=""):
+            return keep.tile(shape, dtype, name=name, align_bytes=64, tag=tag or name)
 
         def bank(b, name):
             return psum.tile([P, S], F32, name=name, tag="bank%d" % b)
@@ -53,29 +54,29 @@ def tile_picked_twcgatebtwice_none_po_kernel(
                     plane[32 * q : 32 * q + 32, :].bitcast(I32), four.unsqueeze(0).to_broadcast([8, 4, four.shape[1]])
                 )
 
-        def deal(name, src, dtype, per_col):
-            dst = sb(name, [P, S * per_col], dtype)
+        def deal(name, src, dtype):
+            dst = sb(name, [P, S], dtype)
             nc.vector.tensor_copy(
-                dst[:].rearrange("p (t m b) -> p t m b", t=PACK, b=per_col),
-                src[:].rearrange("p (m t b) -> p t m b", t=PACK, b=per_col),
+                dst[:].rearrange("p (t m) -> p t m", t=PACK),
+                src[:].rearrange("p (m t) -> p t m", t=PACK),
             )
             return dst
 
         xs = sb("xs", [P, T], U8)
         w2s = sb("w2s", [P, S], U8)
-        w1s = sb("w1s", [P, S], U8)
+        w1s = sb("w1s", [P, S], U8, "w1s_then_two_w")
         l_offs = load_list("l_offs", offs)
         load_scales(nc.sync, xs, x_scales, (0, 1))
-        load_scales(nc.scalar, xs, x_scales, (2, 3))
-        w1w = sb("w1w", [P, 2 * S], U8)
+        w1w = sb("w1w", [P, S], U16)
         nc.scalar.dma_start(w1w[:].bitcast(I32), w1_words[0].bitcast(I32))
+        load_scales(nc.scalar, xs, x_scales, (2, 3))
         l_two = load_list("l_two", two)
         xw = sb("xw", [P, T], U32)
         nc.scalar.dma_start(xw[:].bitcast(I32), x_words[0].rearrange("p n t -> p (n t)").bitcast(I32))
         load_scales(nc.sync, w1s, w1_scales, range(4))
         gain = sb("gain", [P, PACK], F32)
         nc.sync.dma_start(gain[:], gs.rearrange("(p t) o -> p (t o)", t=PACK))
-        w2w = sb("w2w", [P, 2 * S], U8)
+        w2w = sb("w2w", [P, S], U16)
         nc.sync.dma_start(w2w[:].bitcast(I32), w2_words[0].bitcast(I32))
         load_scales(nc.sync, w2s, w2_scales, range(4))
         l_cand = load_list("l_cand", cand)
@@ -88,8 +89,8 @@ def tile_picked_twcgatebtwice_none_po_kernel(
         warm2 = sb("warm2", [P, 2], F32)
         nc.scalar.activation(warm2[:, 0:1], warm[:, 0:1], ACT.Sigmoid)
 
-        def pick(name, table, lst, dtype):
-            g = sb(name, [P, S], dtype)
+        def pick(name, table, lst, dtype, tag=""):
+            g = sb(name, [P, S], dtype, tag)
             nc.vector.tensor_copy(g[:], table[:].indirect(lst[:]))
             return g
 
@@ -99,7 +100,7 @@ def tile_picked_twcgatebtwice_none_po_kernel(
                 acc = bank(first_bank + t, "%s%d" % (name, t))
                 nc.tensor.matmul_mx(
                     out=acc[:],
-                    lhsT=w_words[:, 2 * P * t : 2 * P * (t + 1)].bitcast(FP4X4),
+                    lhsT=w_words[:, P * t : P * (t + 1)].bitcast(FP4X4),
                     lhsT_scale=w_scales[:, P * t : P * (t + 1)],
                     rhs=g_words[:].bitcast(FP8X4),
                     rhs_scale=g_scales[:],
@@ -109,24 +110,23 @@ def tile_picked_twcgatebtwice_none_po_kernel(
                 banks.append(acc)
             return banks
 
+        w1w_d = deal("w1w_d", w1w, U16)
         offs_s = pick("offs_s", xs, l_offs, U8)
-        w1w_d = deal("w1w_d", w1w, U8, 2)
+        w1s_d = deal("w1s_d", w1s, U8)
         offs_w = pick("offs_w", xw, l_offs, U32)
-        w1s_d = deal("w1s_d", w1s, U8, 1)
         y_ps = project("y_ps", PACK, w1w_d, w1s_d, offs_w, offs_s)
         two_s = pick("two_s", xs, l_two, U8)
-        two_w = pick("two_w", xw, l_two, U32)
-        w2w_d = deal("w2w_d", w2w, U8, 2)
-        w2s_d = deal("w2s_d", w2s, U8, 1)
+        w2w_d = deal("w2w_d", w2w, U16)
+        two_w = pick("two_w", xw, l_two, U32, "w1s_then_two_w")
+        w2s_d = deal("w2s_d", w2s, U8)
         d_ps = project("d_ps", 0, w2w_d, w2s_d, two_w, two_s)
         cand_s = pick("cand_s", xs, l_cand, U8)
-        cand_w = pick("cand_w", xw, l_cand, U32)
-        cand_s_d = deal("cand_s_d", cand_s, U8, 1)
-        cand_w_d = deal("cand_w_d", cand_w, U32, 1)
+        cand_w_d = sb("cand_w_d", [P, S], U32)
+        nc.vector.tensor_copy(cand_w_d[:].rearrange("p (t m) -> p m t", t=PACK), xw[:].indirect(l_cand[:]))
+        cand_s_d = deal("cand_s_d", cand_s, U8)
 
         s_win = [sb("s_win%d" % t, [P, 2 * S], F32) for t in range(PACK)]
         y_win = [sb("y_win%d" % t, [P, S], F32) for t in range(PACK)]
-        gated = [sb("gated%d" % t, [P, S], F32) for t in range(PACK)]
         d_win = [sb("d_win%d" % t, [P, S], F32) for t in range(PACK)]
 
         def gate(t, lo, hi):
@@ -136,61 +136,102 @@ def tile_picked_twcgatebtwice_none_po_kernel(
             nc.scalar.activation(y_win[t][:], y_ps[t][:], ACT.Copy, scale=gain[:, t : t + 1])
         for pair in ((0, 1), (2, 3)):
             for t in pair:
-                nc.scalar.copy(d_win[t][:], d_ps[t][:])
+                if t == 2:
+                    nc.vector.tensor_copy(d_win[t][:], d_ps[t][:])
+                else:
+                    nc.scalar.copy(d_win[t][:], d_ps[t][:])
             for t in pair:
                 gate(t, *PIECES[0])
         for lo, hi in PIECES[1:]:
             for t in range(PACK):
                 gate(t, lo, hi)
 
-        def interleave(eng, dst, src, scale):
-            o = dst[:].rearrange("p (c i t) -> p c t i", i=4, t=PACK)
-            i = src[:].rearrange("p t (c i) -> p c t i", i=4)
-            if eng is nc.scalar:
+        def round_and_quantise(src, lo, hi, base, scale, on_scalar, name, codes, scales):
+            grouped = sb(name, [P, PACK * (hi - lo)], BF16)
+            o = grouped[:].rearrange("p (c i t) -> p c t i", i=4, t=PACK)
+            i = src[:, :, lo - base : hi - base].rearrange("p t (c i) -> p c t i", i=4)
+            if on_scalar:
                 nc.scalar.activation(o, i, ACT.Copy, scale=scale)
             else:
                 nc.vector.tensor_scalar(o, i, scale, None, ALU.mult)
+            return lambda: nc.vector.quantize_mx(out=codes[:, lo:hi].bitcast(FP8X4), scales=scales[:, lo:hi], in_=grouped[:])
 
+        def spans(half, t):
+            if half == 0:
+                return ((0, HALF),)
+            return ((HALF, CUT), (CUT, S)) if t == PACK - 1 else ((HALF, S),)
+
+        zz = []
         zq = sb("zq", [P, S], U32)
         zs = sb("zs", [P, S], U8)
-        s_ps = [[bank(t + PACK * h, "s_ps%d_%d" % (t, h)) for h in range(2)] for t in range(PACK)]
         s_plain = [sb("s_plain%d" % t, [P, S], F32) for t in range(PACK)]
-        for n, (lo, hi) in enumerate(PIECES):
-            w = hi - lo
-            z2 = sb("z2_%d" % n, [P, PACK, w], F32)
+
+        def score(t, lo, hi, b):
+            acc = bank(b, "s_ps%d_%d" % (t, lo))
+            nc.tensor.matmul_mx(
+                out=acc[:, 0 : hi - lo],
+                lhsT=cand_w_d[:, P * t : P * (t + 1)].bitcast(FP8X4),
+                lhsT_scale=cand_s_d[:, P * t : P * (t + 1)],
+                rhs=zq[:, lo:hi].bitcast(FP8X4),
+                rhs_scale=zs[:, lo:hi],
+                start=True,
+                stop=True,
+            )
+            return acc[:, 0 : hi - lo]
+
+        for half in range(2):
+            base = half * HALF
+            z2 = sb("z2_%d" % half, [P, PACK, HALF], F32)
+            zz.append(z2)
+            gated = [
+                sb("gated%d_%d" % (half, pair), [P, 2, HALF], F32, "zb_0" if half == 1 and pair == 1 else "")
+                for pair in range(2)
+            ]
             for t in range(PACK):
                 nc.vector.scalar_tensor_tensor(
-                    gated[t][:, lo:hi], s_win[t][:, S + lo : S + hi], 2.0, y_win[t][:, lo:hi], ALU.mult, ALU.mult
+                    gated[t // 2][:, t % 2, :],
+                    s_win[t][:, S + base : S + base + HALF],
+                    2.0,
+                    y_win[t][:, base : base + HALF],
+                    ALU.mult,
+                    ALU.mult,
                 )
             for t in range(PACK):
-                nc.vector.tensor_tensor(
-                    z2[:, t, :], y_win[t][:].indirect(entries(l_n1, lo, hi)), gated[t][:, lo:hi], ALU.subtract
-                )
-            zb = sb("zb_%d" % n, [P, PACK * w], BF16)
-            interleave(nc.vector if n == len(PIECES) - 1 else nc.scalar, zb, z2, -0.5)
-            nc.vector.quantize_mx(out=zq[:, lo:hi].bitcast(FP8X4), scales=zs[:, lo:hi], in_=zb[:])
-            h = lo // HALF
-            for t in range(PACK):
-                nc.tensor.matmul_mx(
-                    out=s_ps[t][h][:, lo - h * HALF : hi - h * HALF],
-                    lhsT=cand_w_d[:, P * t : P * (t + 1)].bitcast(FP8X4),
-                    lhsT_scale=cand_s_d[:, P * t : P * (t + 1)],
-                    rhs=zq[:, lo:hi].bitcast(FP8X4),
-                    rhs_scale=zs[:, lo:hi],
-                    start=True,
-                    stop=True,
-                )
-            if hi % HALF == 0:
+                for lo, hi in spans(half, t):
+                    nc.vector.tensor_tensor(
+                        z2[:, t, lo - base : hi - base],
+                        y_win[t][:].indirect(entries(l_n1, lo, hi)),
+                        gated[t // 2][:, t % 2, lo - base : hi - base],
+                        ALU.subtract,
+                    )
+            if half == 0:
+                round_and_quantise(z2, 0, HALF, base, -0.5, True, "zb_0", zq, zs)()
                 for t in range(PACK):
+                    acc = score(t, 0, HALF, t)
+                    nc.scalar.activation(s_win[t][:, 0:HALF], acc, ACT.Copy, scale=0.03125)
+                    if t == 0:
+                        nc.scalar.activation(s_plain[t][:, 0:HALF], acc, ACT.Copy, scale=0.03125)
+                    else:
+                        nc.sync.dma_start(s_plain[t][:, 0:HALF], s_win[t][:, 0:HALF])
+            else:
+                first = round_and_quantise(z2, HALF, CUT, base, -0.5, True, "zb_1", zq, zs)
+                second = round_and_quantise(z2, CUT, S, base, -0.5, False, "zb_2", zq, zs)
+                first()
+                second()
+                for t in range(PACK):
+                    parts = ((HALF, CUT, PACK), (CUT, S, 0)) if t == 0 else ((HALF, S, PACK + t),)
+                    accs = [(lo, hi, score(t, lo, hi, b)) for lo, hi, b in parts]
                     for dst in (s_win[t], s_plain[t]):
-                        nc.scalar.activation(
-                            dst[:, h * HALF : (h + 1) * HALF], s_ps[t][h][:, 0:HALF], ACT.Copy, scale=0.03125
-                        )
+                        for lo, hi, acc in accs:
+                            nc.scalar.activation(dst[:, lo:hi], acc, ACT.Copy, scale=0.03125)
 
         st_win = [sb("st_win%d" % t, [P, S], F32) for t in range(PACK)]
         st = [sb("st%d" % t, [P, S], F32) for t in range(PACK)]
         for t in range(PACK):
-            nc.vector.tensor_tensor(st_win[t][:], s_win[t][:].indirect(l_n3[:]), s_plain[t][:], ALU.subtract)
+            for lo, hi in PIECES if t == 0 else ((0, S),):
+                nc.vector.tensor_tensor(
+                    st_win[t][:, lo:hi], s_win[t][:].indirect(entries(l_n3, lo, hi)), s_plain[t][:, lo:hi], ALU.subtract
+                )
         for lo, hi in PIECES:
             for t in range(PACK):
                 nc.scalar.activation(st[t][:, lo:hi], st_win[t][:, lo:hi], ACT.Copy, scale=-2.0)
@@ -199,18 +240,27 @@ def tile_picked_twcgatebtwice_none_po_kernel(
         osc = sb("osc", [P, S], U8)
         out_rows = out_0.rearrange("(p t) c -> p t c", t=PACK)
         out_words = out_1[0].rearrange("p n t -> p (n t)").bitcast(I32)
-        for n, (lo, hi) in enumerate(PIECES):
-            w = hi - lo
-            o = sb("o_%d" % n, [P, PACK, w], F32)
+        for half in range(2):
+            base = half * HALF
+            o = sb("o_%d" % half, [P, PACK, HALF], F32)
             for t in range(PACK):
-                nc.vector.tensor_tensor(
-                    o[:, t, :], st_win[t][:].indirect(entries(l_n3, lo, hi)), st[t][:, lo:hi], ALU.add
-                )
-            nc.sync.dma_start(out_rows[:, :, lo:hi], o[:])
-            ob = sb("ob_%d" % n, [P, PACK * w], BF16)
-            interleave(nc.vector if n == len(PIECES) - 1 else nc.scalar, ob, o, 1.0)
-            nc.vector.quantize_mx(out=oq[:, lo:hi].bitcast(FP8X4), scales=osc[:, lo:hi], in_=ob[:])
-            nc.sync.dma_start(out_words[:, lo:hi], oq[:, lo:hi].bitcast(I32))
+                for lo, hi in spans(half, t):
+                    nc.vector.tensor_tensor(
+                        o[:, t, lo - base : hi - base],
+                        st_win[t][:].indirect(entries(l_n3, lo, hi)),
+                        st[t][:, lo:hi],
+                        ALU.add,
+                    )
+                if t % 2:
+                    nc.sync.dma_start(out_rows[:, t - 1 : t + 1, base : base + HALF], o[:, t - 1 : t + 1, :])
+            if half == 0:
+                round_and_quantise(o, 0, HALF, base, 1.0, True, "ob_0", oq, osc)()
+            else:
+                first = round_and_quantise(o, HALF, CUT, base, 1.0, True, "ob_1", oq, osc)
+                second = round_and_quantise(o, CUT, S, base, 1.0, False, "ob_2", oq, osc)
+                first()
+                second()
+            nc.sync.dma_start(out_words[:, base : base + HALF], oq[:, base : base + HALF].bitcast(I32))
         scale_rows = out_2[0].bitcast(I32)
         for q in range(4):
             eng = nc.sync if q % 2 == 0 else nc.scalar

from contextlib import ExitStack

import concourse.mybir as mybir

K, T, S = 512, 2048, 512
FLOPS = 3 * 2 * K * S * S

F32 = mybir.dt.float32
BF16 = mybir.dt.bfloat16
I32 = mybir.dt.int32
U32 = mybir.dt.uint32
U16 = mybir.dt.uint16
U8 = mybir.dt.uint8
FP8X4 = mybir.dt.float8_e4m3fn_x4
FP4X4 = mybir.dt.float4_e2m1fn_x4
ALU = mybir.AluOpType
ACT = mybir.ActivationFunctionType

P = 128
PACK = 4
PER_COL = 16
HALF = S // 2
PIECES = ((0, 256), (256, 512))
CUT = 384


def tile_picked_twcgatebtwice_none_po_kernel(
    tc, x_words, x_scales, w1_words, w1_scales, w2_words, w2_scales, gs, offs, two, n1, n2, cand, n3, out_0, out_1, out_2
):
    nc = tc.nc
    with ExitStack() as ctx:
        keep = ctx.enter_context(tc.tile_pool(name="keep", bufs=1))
        psum = ctx.enter_context(tc.psum_pool(name="psum", bufs=1))

        def sb(name, shape, dtype, tag=""):
            return keep.tile(shape, dtype, name=name, align_bytes=64, tag=tag or name)

        def bank(b, name):
            return psum.tile([P, S], F32, name=name, tag="bank%d" % b)

        def load_list(name, src):
            t = keep.tile([P, S // PER_COL], U16, name=name)
            nc.sync.dma_start(t[:], src)
            return t

        def entries(lst, lo, hi):
            return lst[:, lo // PER_COL : hi // PER_COL]

        def load_scales(eng, plane, src, quadrants):
            rows = src[0].bitcast(I32)
            for q in quadrants:
                four = rows[4 * q : 4 * q + 4, :]
                eng.dma_start(
                    plane[32 * q : 32 * q + 32, :].bitcast(I32), four.unsqueeze(0).to_broadcast([8, 4, four.shape[1]])
                )

        def deal(name, src, dtype):
            dst = sb(name, [P, S], dtype)
            nc.vector.tensor_copy(
                dst[:].rearrange("p (t m) -> p t m", t=PACK),
                src[:].rearrange("p (m t) -> p t m", t=PACK),
            )
            return dst

        xs = sb("xs", [P, T], U8)
        w2s = sb("w2s", [P, S], U8)
        w1s = sb("w1s", [P, S], U8, "w1s_then_two_w")
        l_offs = load_list("l_offs", offs)
        load_scales(nc.sync, xs, x_scales, (0, 1))
        w1w = sb("w1w", [P, S], U16)
        nc.scalar.dma_start(w1w[:].bitcast(I32), w1_words[0].bitcast(I32))
        load_scales(nc.scalar, xs, x_scales, (2, 3))
        l_two = load_list("l_two", two)
        xw = sb("xw", [P, T], U32)
        nc.scalar.dma_start(xw[:].bitcast(I32), x_words[0].rearrange("p n t -> p (n t)").bitcast(I32))
        load_scales(nc.sync, w1s, w1_scales, range(4))
        gain = sb("gain", [P, PACK], F32)
        nc.sync.dma_start(gain[:], gs.rearrange("(p t) o -> p (t o)", t=PACK))
        w2w = sb("w2w", [P, S], U16)
        nc.sync.dma_start(w2w[:].bitcast(I32), w2_words[0].bitcast(I32))
        load_scales(nc.sync, w2s, w2_scales, range(4))
        l_cand = load_list("l_cand", cand)
        l_n2 = load_list("l_n2", n2)
        l_n1 = load_list("l_n1", n1)
        l_n3 = load_list("l_n3", n3)

        warm = sb("warm", [P, 2], F32)
        nc.gpsimd.memset(warm[:, 0:1], 0.0)
        warm2 = sb("warm2", [P, 2], F32)
        nc.scalar.activation(warm2[:, 0:1], warm[:, 0:1], ACT.Sigmoid)

        def pick(name, table, lst, dtype, tag=""):
            g = sb(name, [P, S], dtype, tag)
            nc.vector.tensor_copy(g[:], table[:].indirect(lst[:]))
            return g

        def project(name, first_bank, w_words, w_scales, g_words, g_scales):
            banks = []
            for t in range(PACK):
                acc = bank(first_bank + t, "%s%d" % (name, t))
                nc.tensor.matmul_mx(
                    out=acc[:],
                    lhsT=w_words[:, P * t : P * (t + 1)].bitcast(FP4X4),
                    lhsT_scale=w_scales[:, P * t : P * (t + 1)],
                    rhs=g_words[:].bitcast(FP8X4),
                    rhs_scale=g_scales[:],
                    start=True,
                    stop=True,
                )
                banks.append(acc)
            return banks

        w1w_d = deal("w1w_d", w1w, U16)
        offs_s = pick("offs_s", xs, l_offs, U8)
        w1s_d = deal("w1s_d", w1s, U8)
        offs_w = pick("offs_w", xw, l_offs, U32)
        y_ps = project("y_ps", PACK, w1w_d, w1s_d, offs_w, offs_s)
        two_s = pick("two_s", xs, l_two, U8)
        w2w_d = deal("w2w_d", w2w, U16)
        two_w = pick("two_w", xw, l_two, U32, "w1s_then_two_w")
        w2s_d = deal("w2s_d", w2s, U8)
        d_ps = project("d_ps", 0, w2w_d, w2s_d, two_w, two_s)
        cand_s = pick("cand_s", xs, l_cand, U8)
        cand_w_d = sb("cand_w_d", [P, S], U32)
        nc.vector.tensor_copy(cand_w_d[:].rearrange("p (t m) -> p m t", t=PACK), xw[:].indirect(l_cand[:]))
        cand_s_d = deal("cand_s_d", cand_s, U8)

        s_win = [sb("s_win%d" % t, [P, 2 * S], F32) for t in range(PACK)]
        y_win = [sb("y_win%d" % t, [P, S], F32) for t in range(PACK)]
        d_win = [sb("d_win%d" % t, [P, S], F32) for t in range(PACK)]

        def gate(t, lo, hi):
            nc.scalar.activation(s_win[t][:, S + lo : S + hi], d_win[t][:].indirect(entries(l_n2, lo, hi)), ACT.Sigmoid)

        for t in range(PACK):
            nc.scalar.activation(y_win[t][:], y_ps[t][:], ACT.Copy, scale=gain[:, t : t + 1])
        for pair in ((0, 1), (2, 3)):
            for t in pair:
                if t == 2:
                    nc.vector.tensor_copy(d_win[t][:], d_ps[t][:])
                else:
                    nc.scalar.copy(d_win[t][:], d_ps[t][:])
            for t in pair:
                gate(t, *PIECES[0])
        for lo, hi in PIECES[1:]:
            for t in range(PACK):
                gate(t, lo, hi)

        def round_and_quantise(src, lo, hi, base, scale, on_scalar, name, codes, scales):
            grouped = sb(name, [P, PACK * (hi - lo)], BF16)
            o = grouped[:].rearrange("p (c i t) -> p c t i", i=4, t=PACK)
            i = src[:, :, lo - base : hi - base].rearrange("p t (c i) -> p c t i", i=4)
            if on_scalar:
                nc.scalar.activation(o, i, ACT.Copy, scale=scale)
            else:
                nc.vector.tensor_scalar(o, i, scale, None, ALU.mult)
            return lambda: nc.vector.quantize_mx(out=codes[:, lo:hi].bitcast(FP8X4), scales=scales[:, lo:hi], in_=grouped[:])

        def spans(half, t):
            if half == 0:
                return ((0, HALF),)
            return ((HALF, CUT), (CUT, S)) if t == PACK - 1 else ((HALF, S),)

        zz = []
        zq = sb("zq", [P, S], U32)
        zs = sb("zs", [P, S], U8)
        s_plain = [sb("s_plain%d" % t, [P, S], F32) for t in range(PACK)]

        def score(t, lo, hi, b):
            acc = bank(b, "s_ps%d_%d" % (t, lo))
            nc.tensor.matmul_mx(
                out=acc[:, 0 : hi - lo],
                lhsT=cand_w_d[:, P * t : P * (t + 1)].bitcast(FP8X4),
                lhsT_scale=cand_s_d[:, P * t : P * (t + 1)],
                rhs=zq[:, lo:hi].bitcast(FP8X4),
                rhs_scale=zs[:, lo:hi],
                start=True,
                stop=True,
            )
            return acc[:, 0 : hi - lo]

        for half in range(2):
            base = half * HALF
            z2 = sb("z2_%d" % half, [P, PACK, HALF], F32)
            zz.append(z2)
            gated = [
                sb("gated%d_%d" % (half, pair), [P, 2, HALF], F32, "zb_0" if half == 1 and pair == 1 else "")
                for pair in range(2)
            ]
            for t in range(PACK):
                nc.vector.scalar_tensor_tensor(
                    gated[t // 2][:, t % 2, :],
                    s_win[t][:, S + base : S + base + HALF],
                    2.0,
                    y_win[t][:, base : base + HALF],
                    ALU.mult,
                    ALU.mult,
                )
            for t in range(PACK):
                for lo, hi in spans(half, t):
                    nc.vector.tensor_tensor(
                        z2[:, t, lo - base : hi - base],
                        y_win[t][:].indirect(entries(l_n1, lo, hi)),
                        gated[t // 2][:, t % 2, lo - base : hi - base],
                        ALU.subtract,
                    )
            if half == 0:
                round_and_quantise(z2, 0, HALF, base, -0.5, True, "zb_0", zq, zs)()
                for t in range(PACK):
                    acc = score(t, 0, HALF, t)
                    nc.scalar.activation(s_win[t][:, 0:HALF], acc, ACT.Copy, scale=0.03125)
                    if t == 0:
                        nc.scalar.activation(s_plain[t][:, 0:HALF], acc, ACT.Copy, scale=0.03125)
                    else:
                        nc.sync.dma_start(s_plain[t][:, 0:HALF], s_win[t][:, 0:HALF])
            else:
                first = round_and_quantise(z2, HALF, CUT, base, -0.5, True, "zb_1", zq, zs)
                second = round_and_quantise(z2, CUT, S, base, -0.5, False, "zb_2", zq, zs)
                first()
                second()
                for t in range(PACK):
                    parts = ((HALF, CUT, PACK), (CUT, S, 0)) if t == 0 else ((HALF, S, PACK + t),)
                    accs = [(lo, hi, score(t, lo, hi, b)) for lo, hi, b in parts]
                    for dst in (s_win[t], s_plain[t]):
                        for lo, hi, acc in accs:
                            nc.scalar.activation(dst[:, lo:hi], acc, ACT.Copy, scale=0.03125)

        st_win = [sb("st_win%d" % t, [P, S], F32) for t in range(PACK)]
        st = [sb("st%d" % t, [P, S], F32) for t in range(PACK)]
        for t in range(PACK):
            for lo, hi in PIECES if t == 0 else ((0, S),):
                nc.vector.tensor_tensor(
                    st_win[t][:, lo:hi], s_win[t][:].indirect(entries(l_n3, lo, hi)), s_plain[t][:, lo:hi], ALU.subtract
                )
        for lo, hi in PIECES:
            for t in range(PACK):
                nc.scalar.activation(st[t][:, lo:hi], st_win[t][:, lo:hi], ACT.Copy, scale=-2.0)

        oq = sb("oq", [P, S], U32)
        osc = sb("osc", [P, S], U8)
        out_rows = out_0.rearrange("(p t) c -> p t c", t=PACK)
        out_words = out_1[0].rearrange("p n t -> p (n t)").bitcast(I32)
        for half in range(2):
            base = half * HALF
            o = sb("o_%d" % half, [P, PACK, HALF], F32)
            for t in range(PACK):
                for lo, hi in spans(half, t):
                    nc.vector.tensor_tensor(
                        o[:, t, lo - base : hi - base],
                        st_win[t][:].indirect(entries(l_n3, lo, hi)),
                        st[t][:, lo:hi],
                        ALU.add,
                    )
                if t % 2:
                    nc.sync.dma_start(out_rows[:, t - 1 : t + 1, base : base + HALF], o[:, t - 1 : t + 1, :])
            if half == 0:
                round_and_quantise(o, 0, HALF, base, 1.0, True, "ob_0", oq, osc)()
            else:
                first = round_and_quantise(o, HALF, CUT, base, 1.0, True, "ob_1", oq, osc)
                second = round_and_quantise(o, CUT, S, base, 1.0, False, "ob_2", oq, osc)
                first()
                second()
            nc.sync.dma_start(out_words[:, base : base + HALF], oq[:, base : base + HALF].bitcast(I32))
        scale_rows = out_2[0].bitcast(I32)
        for q in range(4):
            eng = nc.sync if q % 2 == 0 else nc.scalar
            eng.dma_start(scale_rows[4 * q : 4 * q + 4, :], osc[32 * q : 32 * q + 4, :].bitcast(I32))
